import numpy as np
import ml_dtypes


def mxq(x, axis, fmt="e4m3"):
    dtype, down = {"e4m3": (ml_dtypes.float8_e4m3fn, 7), "e5m2": (ml_dtypes.float8_e5m2, 14)}[fmt]
    v = np.moveaxis(np.asarray(x, np.float32).astype(ml_dtypes.bfloat16).astype(np.float64), axis, -1)
    blocks = v.reshape(v.shape[:-1] + (-1, 32))
    amax = np.abs(blocks).max(-1, keepdims=True)
    byte = np.maximum(np.where(amax > 0, np.frexp(amax)[1] - 1 + 127, 0) - down, 1)
    scale = np.exp2(byte - 127.0)
    codes = (blocks / scale).astype(np.float32).astype(dtype).astype(np.float64)
    return np.moveaxis((codes * scale).reshape(v.shape), -1, axis)


WIDE = False


def mx_kscale(k):
    if not WIDE:
        return np.ones(k)
    levels = np.array([10, -10, 5, -5, 0])
    if k % 512:
        return np.exp2(np.random.permutation(np.resize(levels, k // 32))).repeat(32)
    a = np.empty((k // 512, 16))
    for p in range(k // 512):
        a[p, :8] = np.random.permutation(np.resize(levels, 8))
        for g in range(8):
            far = levels[np.abs(levels - a[p, g]) >= 10]
            a[p, g + 8] = far[np.random.randint(len(far))]
    return np.exp2(a.ravel()).repeat(32)


def f64(x):
    return np.asarray(x).astype(np.float64)


def striped(idx):
    return np.tile(idx.reshape(-1, 16).T, (8, 1)).astype(np.uint16)


def unstriped(offs):
    return offs[:16].T.reshape(-1).astype(np.int64)


E2M1 = np.array([0.0, 0.5, 1.0, 1.5, 2.0, 3.0, 4.0, 6.0, -0.0, -0.5, -1.0, -1.5, -2.0, -3.0, -4.0, -6.0])


def pack_weight(w, fmt):
    k, n = w.shape
    w = f64(np.asarray(w, np.float32).astype(ml_dtypes.bfloat16)).reshape(k // 32, 32, n)
    amax = np.abs(w).max(1)
    if fmt == "e4m3":
        byte = np.frexp(amax)[1] - 1 + 127 - 7
    else:
        mant, ex = np.frexp(amax / 6.0)
        byte = np.where(mant > 0.5, ex, ex - 1) + 127
    byte = np.clip(np.where(amax > 0, byte, 1), 1, 254)
    scaled = (w * np.exp2(127.0 - byte)[:, None, :]).reshape(k, n).astype(np.float32)
    by_word = np.ascontiguousarray(scaled.reshape(k // 512, 128, 4, n).transpose(0, 1, 3, 2))
    if fmt == "e4m3":
        words = by_word.astype(ml_dtypes.float8_e4m3fn).view(np.uint8)
    else:
        c = by_word.astype(ml_dtypes.float4_e2m1fn).view(np.uint8) & 0xF
        words = (c[..., 0::2] | (c[..., 1::2] << 4)).reshape(k // 512, 128, 2 * n)
    return np.ascontiguousarray(words), np.ascontiguousarray(byte.astype(np.uint8).reshape(k // 512, 16, n))


def unpack_weight(words, scales, fmt):
    g, _, n = scales.shape
    words = np.ascontiguousarray(words).reshape(g, 128, n, -1)
    if fmt == "e4m3":
        vals = words.view(ml_dtypes.float8_e4m3fn).astype(np.float64)
    else:
        nib = np.empty((g, 128, n, 4), np.uint8)
        nib[..., 0::2] = words & 0xF
        nib[..., 1::2] = words >> 4
        vals = E2M1[nib]
    vals = vals * np.repeat(np.exp2(scales.astype(np.float64) - 127.0), 8, axis=1)[..., None]
    return vals.transpose(0, 1, 3, 2).reshape(g * 512, n)


def gelu(v):
    return 0.5 * v * (1.0 + np.tanh(np.sqrt(2.0 / np.pi) * (v + 0.044715 * v**3)))


K, H, N, T, TF, S, T2 = 1024, 1024, 512, 2048, 1024, 512, 1024

def setup_inputs():
    n = np.random.standard_normal
    s = mx_kscale(K)[:, None]
    u = mx_kscale(H)[:, None]
    tab_words, tab_scales = pack_weight(n((K, T)) * s, "e4m3")
    tab2_words, tab2_scales = pack_weight(n((K, TF)) * s, "e4m3")
    w2_words, w2_scales = pack_weight(n((K, H)) / np.sqrt(K) / s, "e4m3")
    wa_words, wa_scales = pack_weight(n((H, N)) * 1.1 / np.sqrt(H) / u, "e2m1")
    return {
        "tab_words": tab_words, "tab_scales": tab_scales,
        "tab2_words": tab2_words, "tab2_scales": tab2_scales,
        "offs": striped(np.random.permutation(T)[:S]),
        "offs2": striped(np.random.permutation(TF)[:S]),
        "offs3": striped(np.random.permutation(T2)[:S]),
        "offs4": striped(np.random.permutation(T2)[:S]),
        "w1": (n((K, H)) * 1.2 / np.sqrt(K) / s).astype(np.float32),
        "b1": (n(H) * 0.5 - 0.4).astype(np.float32),
        "gain1": (np.exp(0.3 * n(H)) * u[:, 0]).astype(np.float32),
        "w2_words": w2_words, "w2_scales": w2_scales,
        "fall": (np.exp(0.4 * n(H)) * u[:, 0]).astype(np.float32),
        "wg1": np.exp(0.3 * n((128, S))).astype(np.float32),
        "wg2": np.exp(0.3 * n((128, S))).astype(np.float32),
        "radar": ((n((H, T2)) - 0.4) * u).astype(np.float32),
        "wz": (n((H, N)) / np.sqrt(H) / u).astype(np.float32),
        "wa_words": wa_words, "wa_scales": wa_scales,
    }

def reference(tab_words, tab_scales, tab2_words, tab2_scales, offs, offs2, offs3, offs4, w1, b1, gain1, w2_words, w2_scales, fall, wg1, wg2, radar, wz, wa_words, wa_scales):
    v = unpack_weight(tab_words, tab_scales, "e4m3")[:, unstriped(offs)]
    v2 = unpack_weight(tab2_words, tab2_scales, "e4m3")[:, unstriped(offs2)]
    h1 = np.tanh((mxq(f64(w1), 0, "e4m3").T @ v) + f64(b1)[:, None]) * f64(gain1)[:, None]
    h2 = (unpack_weight(w2_words, w2_scales, "e4m3").T @ v2) * f64(fall)[:, None]
    pa = np.zeros((H, T2))
    pa[:, unstriped(offs3)] = np.tile(f64(wg1), (H // 128, 1)) * h1
    pb = np.zeros((H, T2))
    pb[:, unstriped(offs4)] = np.tile(f64(wg2), (H // 128, 1)) * h2
    z = np.maximum(np.maximum(pa, pb), f64(radar))
    wa = unpack_weight(wa_words, wa_scales, "e2m1")
    return mxq(f64(wz), 0, "e4m3").T @ mxq(z, 0, "e4m3") + wa.T @ mxq(np.abs(z), 0, "e4m3")

@@ -1,0 +1,272 @@
+from contextlib import ExitStack
+
+import concourse.mybir as mybir
+
+K, H, N, T, TF, S, T2 = 1024, 1024, 512, 2048, 1024, 512, 1024
+FLOPS = 2 * (2 * K * H * S + 2 * H * N * T2)
+
+F32 = mybir.dt.float32
+BF16 = mybir.dt.bfloat16
+I32 = mybir.dt.int32
+U32 = mybir.dt.uint32
+U16 = mybir.dt.uint16
+U8 = mybir.dt.uint8
+E4M3 = mybir.dt.float8_e4m3fn_x4
+E2M1 = mybir.dt.float4_e2m1fn_x4
+ACT = mybir.ActivationFunctionType
+ALU = mybir.AluOpType
+
+P = 128
+PACK = 4
+KP = P * PACK
+PASSES = 2
+CHUNK = 256
+PB_PAGES = 5
+PA_PAGES = 2
+
+
+def tile_list_hail_severity_cells_kernel(
+    tc, tab_words, tab_scales, tab2_words, tab2_scales, offs, offs2, offs3, offs4, w1, b1, gain1,
+    w2_words, w2_scales, fall, wg1, wg2, radar, wz, wa_words, wa_scales, out,
+):
+    nc = tc.nc
+    with ExitStack() as ctx:
+        keep = ctx.enter_context(tc.tile_pool(name="keep", bufs=1))
+        ring = ctx.enter_context(tc.tile_pool(name="ring", bufs=1))
+        psum = ctx.enter_context(tc.psum_pool(name="psum", bufs=1))
+
+        def load_list(src, name):
+            t = keep.tile([P, S // 16], U16, name=name)
+            nc.sync.dma_start(t[:], src)
+            return t
+
+        def load_words(src, a, cols, name):
+            t = keep.tile([P, cols.stop - cols.start], U32, name=name, tag=name, align_bytes=64)
+            nc.sync.dma_start(t[:].bitcast(I32), src[a].rearrange("p c i -> p (c i)").bitcast(I32)[:, cols])
+            return t
+
+        def zero_plane(width, name, engine):
+            t = keep.tile([P, width], U8, name=name, align_bytes=64)
+            engine.memset(t[:].bitcast(I32), 0)
+            return t
+
+        def load_packed_scales(t, src):
+            for q in range(4):
+                nc.sync.dma_start(t[32 * q : 32 * q + 8, :].bitcast(I32), src[:, 4 * q : 4 * q + 4, :].bitcast(I32))
+
+        def load_vector(src, name):
+            t = keep.tile([P, PASSES, PACK], F32, name=name)
+            nc.sync.dma_start(t[:], src.rearrange("(b p t) -> p b t", b=PASSES, t=PACK))
+            return t
+
+        def load_dealt(src, name):
+            t = keep.tile([P, PACK, S], F32, name=name)
+            for q in range(4):
+                nc.sync.dma_start(t[32 * q : 32 * q + 32], src.rearrange("(i t) j -> i t j", t=PACK))
+            return t
+
+        def gather(words, scales, lst, name):
+            codes = []
+            for a in range(PASSES):
+                g = keep.tile([P, S], U32, name=name + "_codes%d" % a, align_bytes=64)
+                nc.vector.tensor_copy(g[:], words[a][:].indirect(lst[:]))
+                codes.append(g)
+            gs = keep.tile([P, S], U8, name=name + "_scales", align_bytes=64)
+            nc.vector.tensor_copy(gs[:], scales[:].indirect(lst[:]))
+            return codes, gs
+
+        def deal_columns(dst, src):
+            nc.vector.tensor_copy(
+                dst.rearrange("p (t c i) -> p c t i", t=PACK, i=4),
+                src.rearrange("p (c i t) -> p c t i", t=PACK, i=4),
+            )
+
+        def bank(k, shape):
+            return psum.tile(shape, F32, name="bank%d" % k, tag="bank%d" % k)
+
+        tab2_s = zero_plane(TF, "tab2_s", nc.vector)
+        w2_s = zero_plane(H, "w2_s", nc.gpsimd)
+        tab_s = zero_plane(T, "tab_s", nc.vector)
+        wa_s = zero_plane(PASSES * N, "wa_s", nc.gpsimd)
+        pb = [keep.tile([P, T2], F32, name="pb%d" % i) for i in range(PB_PAGES)]
+        for page in pb:
+            nc.vector.memset(page[:], 0.0)
+
+        l2 = load_list(offs2, "l2")
+        tab2_w = [load_words(tab2_words, a, slice(0, TF), "tab2_w%d" % a) for a in range(PASSES)]
+        load_packed_scales(tab2_s, tab2_scales)
+        w2_w = {(0, a): load_words(w2_words, a, slice(0, KP), "w2_w0%d" % a) for a in range(PASSES)}
+        load_packed_scales(w2_s, w2_scales)
+        l4 = load_list(offs4, "l4")
+        fall_v = load_vector(fall, "fall_v")
+        wg2_t = load_dealt(wg2, "wg2_t")
+        l1 = load_list(offs, "l1")
+        tab_w = [load_words(tab_words, a, slice(0, T), "tab_w%d" % a) for a in range(PASSES)]
+        load_packed_scales(tab_s, tab_scales)
+
+        def load_rows(src, a, cols):
+            raw = ring.tile([P, PACK, KP], F32, name="raw", bufs=3)
+            nc.sync.dma_start(raw[:], src[a * KP : (a + 1) * KP, cols].rearrange("(p j) c -> p j c", j=PACK))
+            return raw
+
+        def quantise(grouped, width, name, pool, bufs):
+            codes = pool.tile([P, width], U32, name=name + "_codes", align_bytes=64, bufs=bufs)
+            scales = pool.tile([P, width], U8, name=name + "_scales", align_bytes=64, bufs=bufs)
+            nc.vector.quantize_mx(out=codes[:].bitcast(E4M3), scales=scales[:], in_=grouped[:])
+            return codes, scales
+
+        def w1_part(b, a):
+            raw = load_rows(w1, a, slice(b * KP, (b + 1) * KP))
+            grouped = ring.tile([P, PACK * KP], BF16, name="grouped", bufs=3, align_bytes=64)
+            dst = grouped[:].rearrange("p (u e m j) -> p u m j e", u=2, e=2, j=PACK)
+            src = raw[:].rearrange("p j (m u e) -> p u m j e", u=2, e=2)
+            for u in range(2):
+                nc.scalar.copy(dst[:, u], src[:, u])
+            return quantise(grouped, KP, "w1_%d%d" % (b, a), keep, 1)
+
+        def wz_part(b):
+            raw = load_rows(wz, b, slice(0, N))
+            grouped = ring.tile([P, PACK * KP], BF16, name="grouped", bufs=3, align_bytes=64)
+            nc.scalar.copy(
+                grouped[:].rearrange("p (c i j) -> p c j i", i=2, j=PACK),
+                raw[:].rearrange("p j (c i) -> p c j i", i=2),
+            )
+            return quantise(grouped, N, "wz_%d" % b, keep, 1)
+
+        def deal_w2(b):
+            codes = []
+            for a in range(PASSES):
+                d = keep.tile([P, KP], U32, name="w2_d%d%d" % (b, a), align_bytes=64)
+                deal_columns(d[:], w2_w[b, a][:])
+                codes.append(d)
+            ds = keep.tile([P, KP], U8, name="w2_ds%d" % b, align_bytes=64)
+            deal_columns(ds[:], w2_s[:, b * KP : (b + 1) * KP])
+            return codes, ds
+
+        def first_product(acc, t, lhs, rhs):
+            cols = slice(t * P, (t + 1) * P)
+            for a in range(PASSES):
+                codes, scales = lhs[a]
+                nc.tensor.matmul_mx(
+                    out=acc[:], lhsT=codes[:, cols].bitcast(E4M3), lhsT_scale=scales[:, cols],
+                    rhs=rhs[0][a][:].bitcast(E4M3), rhs_scale=rhs[1][4 * a : P, :],
+                    start=(a == 0), stop=(a == PASSES - 1),
+                )
+
+        def make_h2(b, t, w2_d):
+            acc = bank(t, [P, S])
+            first_product(acc, t, [(w2_d[0][a], w2_d[1][4 * a : P]) for a in range(PASSES)], v2)
+            h = ring.tile([P, S], F32, name="h2", bufs=4)
+            nc.scalar.activation(h[:], acc[:], ACT.Copy, scale=fall_v[:, b, t : t + 1])
+            return h
+
+        def make_h1(b, t, w1_q):
+            acc = bank(4 + t, [P, S])
+            first_product(acc, t, w1_q, v1)
+            h = ring.tile([P, S], F32, name="h1", bufs=5)
+            nc.scalar.activation(h[:], acc[:], ACT.Tanh, bias=b1_v[:, b, t : t + 1])
+            nc.scalar.activation(h[:], h[:], ACT.Copy, scale=gain_v[:, b, t : t + 1])
+            return h
+
+        def place(page, lst, h, wg, t):
+            nc.vector.tensor_tensor(page[:].indirect(lst[:]), h[:], wg[:, t, :], ALU.mult)
+
+        def place_b(b, t, w2_d):
+            place(pb[(PACK * b + t) % PB_PAGES], l4, make_h2(b, t, w2_d), wg2_t, t)
+
+        def place_a(b, t, h):
+            place(pa[(PACK * b + t) % PA_PAGES], l3, h, wg1_t, t)
+
+        def page_max(both, b, t):
+            s = PACK * b + t
+            nc.vector.tensor_tensor(both[:, t, :], pa[s % PA_PAGES][:], pb[s % PB_PAGES][:], ALU.max)
+
+        def load_radar(b):
+            r = ring.tile([P, PACK, T2], F32, name="radar_t", bufs=1)
+            nc.sync.dma_start(r[:], radar[b * KP : (b + 1) * KP, :].rearrange("(p j) m -> p j m", j=PACK))
+            return r
+
+        def second_stage(b, c, both, radar_t, accs):
+            cols = slice(c * CHUNK, (c + 1) * CHUNK)
+            z = ring.tile([P, PACK * CHUNK], BF16, name="z", bufs=3, align_bytes=64)
+            nc.vector.tensor_tensor(
+                z[:].rearrange("p (c i t) -> p c t i", i=2, t=PACK),
+                both[:, :, cols].rearrange("p t (c i) -> p c t i", i=2),
+                radar_t[:, :, cols].rearrange("p t (c i) -> p c t i", i=2),
+                ALU.max,
+            )
+            size = ring.tile([P, PACK * CHUNK], BF16, name="size", bufs=3, align_bytes=64)
+            nc.scalar.activation(size[:], z[:], ACT.Abs)
+            zq = quantise(z, CHUNK, "zq", ring, 4)
+            for g in range(N // P):
+                nc.tensor.matmul_mx(
+                    out=accs[g // 2][:, g % 2, :],
+                    lhsT=wz_q[b][0][:, g * P : (g + 1) * P].bitcast(E4M3), lhsT_scale=wz_q[b][1][:, g * P : (g + 1) * P],
+                    rhs=zq[0][:].bitcast(E4M3), rhs_scale=zq[1][:],
+                    start=(b == 0 and g % 2 == 0), stop=False,
+                )
+            sq = quantise(size, CHUNK, "sq", ring, 4)
+            for g in range(N // P):
+                nc.tensor.matmul_mx(
+                    out=accs[g // 2][:, g % 2, :],
+                    lhsT=wa_w[:, b, 2 * g * P : 2 * (g + 1) * P].bitcast(E2M1),
+                    lhsT_scale=wa_s[:, b * N + g * P : b * N + (g + 1) * P],
+                    rhs=sq[0][:].bitcast(E4M3), rhs_scale=sq[1][:],
+                    start=False, stop=(b == PASSES - 1 and g % 2 == 1),
+                )
+
+        v2 = gather(tab2_w, tab2_s, l2, "v2")
+        w2_d = deal_w2(0)
+        pa = [keep.tile([P, T2], F32, name="pa%d" % i, tag="tab2_w%d" % i, align_bytes=64) for i in range(PA_PAGES)]
+        for page in pa:
+            nc.gpsimd.memset(page[:], 0.0)
+        for t in range(PACK):
+            place_b(0, t, w2_d)
+        v1 = gather(tab_w, tab_s, l1, "v1")
+
+        w1_q = [w1_part(0, a) for a in range(PASSES)]
+        b1_v = load_vector(b1, "b1_v")
+        gain_v = load_vector(gain1, "gain_v")
+        l3 = load_list(offs3, "l3")
+        wg1_t = load_dealt(wg1, "wg1_t")
+        for a in range(PASSES):
+            w2_w[1, a] = load_words(w2_words, a, slice(KP, H), "w2_w1%d" % a)
+        w2_d = deal_w2(1)
+
+        both = ring.tile([P, PACK, T2], F32, name="both", bufs=1)
+        for t in range(PACK):
+            place_a(0, t, make_h1(0, t, w1_q))
+            place_b(1, t, w2_d)
+            page_max(both, 0, t)
+
+        w1_q = [w1_part(1, a) for a in range(PASSES)]
+        h1 = [make_h1(1, t, w1_q) for t in range(PACK)]
+        radar_t = load_radar(0)
+        wz_q = [wz_part(b) for b in range(PASSES)]
+        wa_w = keep.tile([P, PASSES, 2 * N], U8, name="wa_w", align_bytes=64)
+        nc.sync.dma_start(wa_w[:].bitcast(I32), wa_words.rearrange("a p c -> p a c").bitcast(I32))
+        for q in range(4):
+            nc.sync.dma_start(
+                wa_s[32 * q : 32 * q + 4, :].rearrange("r (a c) -> r a c", a=PASSES).bitcast(I32),
+                wa_scales[:, 4 * q : 4 * q + 4, :].rearrange("a r c -> r a c").bitcast(I32),
+            )
+
+        place_a(1, 0, h1[0])
+        accs = [[bank(2 * c + i, [P, 2, CHUNK]) for i in range(2)] for c in range(T2 // CHUNK)]
+        for c in range(T2 // CHUNK):
+            second_stage(0, c, both, radar_t, accs[c])
+
+        radar_t = load_radar(1)
+        both = ring.tile([P, PACK, T2], F32, name="both", bufs=1)
+        for t in range(PACK):
+            if t + 1 < PACK:
+                place_a(1, t + 1, h1[t + 1])
+            page_max(both, 1, t)
+
+        out_v = out.rearrange("(g p) m -> p g m", p=P)
+        for c in range(T2 // CHUNK):
+            second_stage(1, c, both, radar_t, accs[c])
+            for i in range(2):
+                res = ring.tile([P, 2, CHUNK], F32, name="res", bufs=4)
+                nc.scalar.copy(res[:], accs[c][i][:])
+                nc.sync.dma_start(out_v[:, 2 * i : 2 * i + 2, c * CHUNK : (c + 1) * CHUNK], res[:])

@@ -20,9 +20,10 @@ P = 128
 PACK = 4
 KP = P * PACK
 PASSES = 2
-CHUNK = 256
+WIDTHS = (256, 256, 256, 128, 128)
 PB_PAGES = 5
 PA_PAGES = 2
+PB_OF = (0, 1, 2, 3, 4, 0, 1, 0)
 
 
 def tile_list_hail_severity_cells_kernel(
@@ -45,18 +46,25 @@ def tile_list_hail_severity_cells_kernel(
             nc.sync.dma_start(t[:].bitcast(I32), src[a].rearrange("p c i -> p (c i)").bitcast(I32)[:, cols])
             return t
 
+        def load_w2(b):
+            t = keep.tile([P, PASSES, KP], U32, name="w2_w%d" % b, align_bytes=64)
+            words = w2_words.rearrange("a p c i -> p a (c i)").bitcast(I32)
+            nc.sync.dma_start(t[:].bitcast(I32), words[:, :, b * KP : (b + 1) * KP])
+            return t
+
         def zero_plane(width, name, engine):
             t = keep.tile([P, width], U8, name=name, align_bytes=64)
             engine.memset(t[:].bitcast(I32), 0)
             return t
 
-        def load_packed_scales(t, src):
+        def load_packed_scales(t, src, queue):
             for q in range(4):
-                nc.sync.dma_start(t[32 * q : 32 * q + 8, :].bitcast(I32), src[:, 4 * q : 4 * q + 4, :].bitcast(I32))
+                queue.dma_start(t[32 * q : 32 * q + 8, :].bitcast(I32), src[:, 4 * q : 4 * q + 4, :].bitcast(I32))
 
-        def load_vector(src, name):
-            t = keep.tile([P, PASSES, PACK], F32, name=name)
-            nc.sync.dma_start(t[:], src.rearrange("(b p t) -> p b t", b=PASSES, t=PACK))
+        def load_vector(src, name, queue):
+            blocks = src.shape[0] // KP
+            t = keep.tile([P, blocks, PACK], F32, name=name)
+            queue.dma_start(t[:], src.rearrange("(b p t) -> p b t", b=blocks, t=PACK))
             return t
 
         def load_dealt(src, name):
@@ -65,15 +73,17 @@ def tile_list_hail_severity_cells_kernel(
                 nc.sync.dma_start(t[32 * q : 32 * q + 32], src.rearrange("(i t) j -> i t j", t=PACK))
             return t
 
-        def gather(words, scales, lst, name):
-            codes = []
+        def gathered(name):
+            codes = [keep.tile([P, S], U32, name=name + "_codes%d" % a, align_bytes=64) for a in range(PASSES)]
+            return codes, keep.tile([P, S], U8, name=name + "_scales", align_bytes=64)
+
+        def entries(lst, js):
+            return lst[:, js.start // 16 : js.stop // 16]
+
+        def gather(dst, words, scales, lst, js):
             for a in range(PASSES):
-                g = keep.tile([P, S], U32, name=name + "_codes%d" % a, align_bytes=64)
-                nc.vector.tensor_copy(g[:], words[a][:].indirect(lst[:]))
-                codes.append(g)
-            gs = keep.tile([P, S], U8, name=name + "_scales", align_bytes=64)
-            nc.vector.tensor_copy(gs[:], scales[:].indirect(lst[:]))
-            return codes, gs
+                nc.vector.tensor_copy(dst[0][a][:, js], words[a][:].indirect(entries(lst, js)))
+            nc.vector.tensor_copy(dst[1][:, js], scales[:].indirect(entries(lst, js)))
 
         def deal_columns(dst, src):
             nc.vector.tensor_copy(
@@ -87,22 +97,24 @@ def tile_list_hail_severity_cells_kernel(
         tab2_s = zero_plane(TF, "tab2_s", nc.vector)
         w2_s = zero_plane(H, "w2_s", nc.gpsimd)
         tab_s = zero_plane(T, "tab_s", nc.vector)
-        wa_s = zero_plane(PASSES * N, "wa_s", nc.gpsimd)
+        wa_s = zero_plane(PASSES * N, "wa_s", nc.vector)
         pb = [keep.tile([P, T2], F32, name="pb%d" % i) for i in range(PB_PAGES)]
-        for page in pb:
+        pa = [keep.tile([P, T2], F32, name="pa0")]
+        for page in pb + pa:
             nc.vector.memset(page[:], 0.0)
 
+        fall_v = [load_vector(fall[0:KP], "fall_v0", nc.gpsimd)]
         l2 = load_list(offs2, "l2")
         tab2_w = [load_words(tab2_words, a, slice(0, TF), "tab2_w%d" % a) for a in range(PASSES)]
-        load_packed_scales(tab2_s, tab2_scales)
-        w2_w = {(0, a): load_words(w2_words, a, slice(0, KP), "w2_w0%d" % a) for a in range(PASSES)}
-        load_packed_scales(w2_s, w2_scales)
+        load_packed_scales(tab2_s, tab2_scales, nc.scalar)
+        w2_w = [load_w2(0)]
+        load_packed_scales(w2_s, w2_scales, nc.scalar)
         l4 = load_list(offs4, "l4")
-        fall_v = load_vector(fall, "fall_v")
         wg2_t = load_dealt(wg2, "wg2_t")
+        w2_w.append(load_w2(1))
         l1 = load_list(offs, "l1")
         tab_w = [load_words(tab_words, a, slice(0, T), "tab_w%d" % a) for a in range(PASSES)]
-        load_packed_scales(tab_s, tab_scales)
+        load_packed_scales(tab_s, tab_scales, nc.sync)
 
         def load_rows(src, a, cols):
             raw = ring.tile([P, PACK, KP], F32, name="raw", bufs=3)
@@ -117,7 +129,7 @@ def tile_list_hail_severity_cells_kernel(
 
         def w1_part(b, a):
             raw = load_rows(w1, a, slice(b * KP, (b + 1) * KP))
-            grouped = ring.tile([P, PACK * KP], BF16, name="grouped", bufs=3, align_bytes=64)
+            grouped = ring.tile([P, PACK * KP], BF16, name="grouped", bufs=4, align_bytes=64)
             dst = grouped[:].rearrange("p (u e m j) -> p u m j e", u=2, e=2, j=PACK)
             src = raw[:].rearrange("p j (m u e) -> p u m j e", u=2, e=2)
             for u in range(2):
@@ -126,7 +138,7 @@ def tile_list_hail_severity_cells_kernel(
 
         def wz_part(b):
             raw = load_rows(wz, b, slice(0, N))
-            grouped = ring.tile([P, PACK * KP], BF16, name="grouped", bufs=3, align_bytes=64)
+            grouped = ring.tile([P, PACK * KP], BF16, name="grouped", bufs=4, align_bytes=64)
             nc.scalar.copy(
                 grouped[:].rearrange("p (c i j) -> p c j i", i=2, j=PACK),
                 raw[:].rearrange("p j (c i) -> p c j i", i=2),
@@ -137,111 +149,132 @@ def tile_list_hail_severity_cells_kernel(
             codes = []
             for a in range(PASSES):
                 d = keep.tile([P, KP], U32, name="w2_d%d%d" % (b, a), align_bytes=64)
-                deal_columns(d[:], w2_w[b, a][:])
+                deal_columns(d[:], w2_w[b][:, a, :])
                 codes.append(d)
             ds = keep.tile([P, KP], U8, name="w2_ds%d" % b, align_bytes=64)
             deal_columns(ds[:], w2_s[:, b * KP : (b + 1) * KP])
             return codes, ds
 
-        def first_product(acc, t, lhs, rhs):
+        def first_product(acc, t, lhs, rhs, js):
             cols = slice(t * P, (t + 1) * P)
             for a in range(PASSES):
                 codes, scales = lhs[a]
                 nc.tensor.matmul_mx(
                     out=acc[:], lhsT=codes[:, cols].bitcast(E4M3), lhsT_scale=scales[:, cols],
-                    rhs=rhs[0][a][:].bitcast(E4M3), rhs_scale=rhs[1][4 * a : P, :],
+                    rhs=rhs[0][a][:, js].bitcast(E4M3), rhs_scale=rhs[1][4 * a : P, js],
                     start=(a == 0), stop=(a == PASSES - 1),
                 )
 
-        def make_h2(b, t, w2_d):
-            acc = bank(t, [P, S])
-            first_product(acc, t, [(w2_d[0][a], w2_d[1][4 * a : P]) for a in range(PASSES)], v2)
-            h = ring.tile([P, S], F32, name="h2", bufs=4)
-            nc.scalar.activation(h[:], acc[:], ACT.Copy, scale=fall_v[:, b, t : t + 1])
+        def make_h2(b, t, w2_d, js, k):
+            acc = bank(k, [P, js.stop - js.start])
+            first_product(acc, t, [(w2_d[0][a], w2_d[1][4 * a : P]) for a in range(PASSES)], v2, js)
+            h = ring.tile([P, js.stop - js.start], F32, name="h2", bufs=4)
+            nc.scalar.activation(h[:], acc[:], ACT.Copy, scale=fall_v[b][:, 0, t : t + 1])
             return h
 
-        def make_h1(b, t, w1_q):
-            acc = bank(4 + t, [P, S])
-            first_product(acc, t, w1_q, v1)
+        def make_h1(b, t, w1_q, k):
+            acc = bank(k, [P, S])
+            first_product(acc, t, w1_q, v1, whole)
             h = ring.tile([P, S], F32, name="h1", bufs=5)
             nc.scalar.activation(h[:], acc[:], ACT.Tanh, bias=b1_v[:, b, t : t + 1])
             nc.scalar.activation(h[:], h[:], ACT.Copy, scale=gain_v[:, b, t : t + 1])
             return h
 
-        def place(page, lst, h, wg, t):
-            nc.vector.tensor_tensor(page[:].indirect(lst[:]), h[:], wg[:, t, :], ALU.mult)
+        def place(page, lst, h, wg, t, js):
+            nc.vector.tensor_tensor(page[:].indirect(entries(lst, js)), h[:], wg[:, t, js], ALU.mult)
 
-        def place_b(b, t, w2_d):
-            place(pb[(PACK * b + t) % PB_PAGES], l4, make_h2(b, t, w2_d), wg2_t, t)
+        def place_b(b, t, h, js):
+            place(pb[PB_OF[PACK * b + t]], l4, h, wg2_t, t, js)
 
         def place_a(b, t, h):
-            place(pa[(PACK * b + t) % PA_PAGES], l3, h, wg1_t, t)
+            place(pa[(PACK * b + t) % PA_PAGES], l3, h, wg1_t, t, whole)
 
-        def page_max(both, b, t):
+        def page_max(both, b, t, cols=slice(0, T2)):
             s = PACK * b + t
-            nc.vector.tensor_tensor(both[:, t, :], pa[s % PA_PAGES][:], pb[s % PB_PAGES][:], ALU.max)
+            nc.vector.tensor_tensor(both[:, t, cols], pa[s % PA_PAGES][:, cols], pb[PB_OF[s]][:, cols], ALU.max)
 
-        def load_radar(b):
-            r = ring.tile([P, PACK, T2], F32, name="radar_t", bufs=1)
-            nc.sync.dma_start(r[:], radar[b * KP : (b + 1) * KP, :].rearrange("(p j) m -> p j m", j=PACK))
-            return r
+        def load_radar(b, tags):
+            parts = []
+            for i in range(2):
+                r = keep.tile([P, PACK, KP], F32, name="radar%d%d" % (b, i), tag=tags % i, align_bytes=64)
+                rows = radar[b * KP : (b + 1) * KP, i * KP : (i + 1) * KP]
+                nc.sync.dma_start(r[:], rows.rearrange("(p j) m -> p j m", j=PACK))
+                parts.append(r)
+            return parts
 
-        def second_stage(b, c, both, radar_t, accs):
-            cols = slice(c * CHUNK, (c + 1) * CHUNK)
-            z = ring.tile([P, PACK * CHUNK], BF16, name="z", bufs=3, align_bytes=64)
+        def target(cols, g):
+            per_bank = KP // (cols.stop - cols.start)
+            return accs[cols.start][g // per_bank][:, g % per_bank, :], g % per_bank == 0, g % per_bank == per_bank - 1
+
+        def second_stage(b, cols, both, radar_t):
+            width = cols.stop - cols.start
+            z = ring.tile([P, PACK * width], BF16, name="z", bufs=3, align_bytes=64)
             nc.vector.tensor_tensor(
                 z[:].rearrange("p (c i t) -> p c t i", i=2, t=PACK),
                 both[:, :, cols].rearrange("p t (c i) -> p c t i", i=2),
-                radar_t[:, :, cols].rearrange("p t (c i) -> p c t i", i=2),
+                radar_t[cols.start // KP][:, :, cols.start % KP : cols.start % KP + width].rearrange("p t (c i) -> p c t i", i=2),
                 ALU.max,
             )
-            size = ring.tile([P, PACK * CHUNK], BF16, name="size", bufs=3, align_bytes=64)
-            nc.scalar.activation(size[:], z[:], ACT.Abs)
-            zq = quantise(z, CHUNK, "zq", ring, 4)
+            size = ring.tile([P, PACK * width], BF16, name="size", bufs=3, align_bytes=64)
+            if b == PASSES - 1 and cols.start >= T2 // 2:
+                nc.vector.scalar_tensor_tensor(size[:], z[:], -1.0, z[:], ALU.mult, ALU.max)
+            else:
+                nc.scalar.activation(size[:], z[:], ACT.Abs)
+            zq = quantise(z, width, "zq", ring, 3)
             for g in range(N // P):
+                acc, first, last = target(cols, g)
                 nc.tensor.matmul_mx(
-                    out=accs[g // 2][:, g % 2, :],
+                    out=acc,
                     lhsT=wz_q[b][0][:, g * P : (g + 1) * P].bitcast(E4M3), lhsT_scale=wz_q[b][1][:, g * P : (g + 1) * P],
                     rhs=zq[0][:].bitcast(E4M3), rhs_scale=zq[1][:],
-                    start=(b == 0 and g % 2 == 0), stop=False,
+                    start=(b == 0 and first), stop=False,
                 )
-            sq = quantise(size, CHUNK, "sq", ring, 4)
+            sq = quantise(size, width, "sq", ring, 3)
             for g in range(N // P):
+                acc, first, last = target(cols, g)
                 nc.tensor.matmul_mx(
-                    out=accs[g // 2][:, g % 2, :],
+                    out=acc,
                     lhsT=wa_w[:, b, 2 * g * P : 2 * (g + 1) * P].bitcast(E2M1),
                     lhsT_scale=wa_s[:, b * N + g * P : b * N + (g + 1) * P],
                     rhs=sq[0][:].bitcast(E4M3), rhs_scale=sq[1][:],
-                    start=False, stop=(b == PASSES - 1 and g % 2 == 1),
+                    start=False, stop=(b == PASSES - 1 and last),
                 )
 
-        v2 = gather(tab2_w, tab2_s, l2, "v2")
+        whole = slice(0, S)
+        halves = [slice(0, S // 2), slice(S // 2, S)]
+        v2 = gathered("v2")
+        gather(v2, tab2_w, tab2_s, l2, halves[0])
         w2_d = deal_w2(0)
-        pa = [keep.tile([P, T2], F32, name="pa%d" % i, tag="tab2_w%d" % i, align_bytes=64) for i in range(PA_PAGES)]
-        for page in pa:
-            nc.gpsimd.memset(page[:], 0.0)
-        for t in range(PACK):
-            place_b(0, t, w2_d)
-        v1 = gather(tab_w, tab_s, l1, "v1")
+        h_first = make_h2(0, 0, w2_d, halves[0], 0)
+        gather(v2, tab2_w, tab2_s, l2, halves[1])
+        place_b(0, 0, h_first, halves[0])
+        place_b(0, 0, make_h2(0, 0, w2_d, halves[1], 1), halves[1])
+        pa.append(keep.tile([P, T2], F32, name="pa1", tag="tab2_w0", align_bytes=64))
+        nc.gpsimd.memset(pa[1][:], 0.0)
+        for t in range(1, PACK):
+            place_b(0, t, make_h2(0, t, w2_d, whole, t + 1), whole)
+        w2_d = deal_w2(1)
+        v1 = gathered("v1")
+        gather(v1, tab_w, tab_s, l1, whole)
 
-        w1_q = [w1_part(0, a) for a in range(PASSES)]
-        b1_v = load_vector(b1, "b1_v")
-        gain_v = load_vector(gain1, "gain_v")
+        w1_q = [[w1_part(b, a) for a in range(PASSES)] for b in range(PASSES)]
+        fall_v.append(load_vector(fall[KP:H], "fall_v1", nc.sync))
+        place_b(1, 0, make_h2(1, 0, w2_d, whole, 5), whole)
+        b1_v = load_vector(b1, "b1_v", nc.sync)
+        gain_v = load_vector(gain1, "gain_v", nc.sync)
         l3 = load_list(offs3, "l3")
         wg1_t = load_dealt(wg1, "wg1_t")
-        for a in range(PASSES):
-            w2_w[1, a] = load_words(w2_words, a, slice(KP, H), "w2_w1%d" % a)
-        w2_d = deal_w2(1)
 
         both = ring.tile([P, PACK, T2], F32, name="both", bufs=1)
         for t in range(PACK):
-            place_a(0, t, make_h1(0, t, w1_q))
-            place_b(1, t, w2_d)
+            place_a(0, t, make_h1(0, t, w1_q[0], (6 + t) % 8))
             page_max(both, 0, t)
+            if t + 2 < PACK:
+                place_b(1, t + 1, make_h2(1, t + 1, w2_d, whole, (6 + t) % 8), whole)
+        h2_last = make_h2(1, PACK - 1, w2_d, whole, 0)
 
-        w1_q = [w1_part(1, a) for a in range(PASSES)]
-        h1 = [make_h1(1, t, w1_q) for t in range(PACK)]
-        radar_t = load_radar(0)
+        h1 = [make_h1(1, t, w1_q[1], 2 + t) for t in range(PACK)]
+        radar_t = load_radar(0, "radar%d")
         wz_q = [wz_part(b) for b in range(PASSES)]
         wa_w = keep.tile([P, PASSES, 2 * N], U8, name="wa_w", align_bytes=64)
         nc.sync.dma_start(wa_w[:].bitcast(I32), wa_words.rearrange("a p c -> p a c").bitcast(I32))
@@ -252,21 +285,40 @@ def tile_list_hail_severity_cells_kernel(
             )
 
         place_a(1, 0, h1[0])
-        accs = [[bank(2 * c + i, [P, 2, CHUNK]) for i in range(2)] for c in range(T2 // CHUNK)]
-        for c in range(T2 // CHUNK):
-            second_stage(0, c, both, radar_t, accs[c])
+        chunks = []
+        accs = {}
+        for width in WIDTHS:
+            start = chunks[-1].stop if chunks else 0
+            chunks.append(slice(start, start + width))
+            per_bank = KP // width
+            accs[start] = [bank(start // P + i, [P, per_bank, width]) for i in range(N // P // per_bank)]
+        for cols in chunks:
+            second_stage(0, cols, both, radar_t)
 
-        radar_t = load_radar(1)
+        radar_t = load_radar(1, "tab_w%d")
         both = ring.tile([P, PACK, T2], F32, name="both", bufs=1)
-        for t in range(PACK):
-            if t + 1 < PACK:
-                place_a(1, t + 1, h1[t + 1])
-            page_max(both, 1, t)
+        place_a(1, 1, h1[1])
+        page_max(both, 1, 0)
+        page_max(both, 1, 1)
+        place_a(1, 2, h1[2])
+        place_b(1, 3, h2_last, whole)
+        page_max(both, 1, 2)
+        place_a(1, 3, h1[3])
 
         out_v = out.rearrange("(g p) m -> p g m", p=P)
-        for c in range(T2 // CHUNK):
-            second_stage(1, c, both, radar_t, accs[c])
-            for i in range(2):
-                res = ring.tile([P, 2, CHUNK], F32, name="res", bufs=4)
-                nc.scalar.copy(res[:], accs[c][i][:])
-                nc.sync.dma_start(out_v[:, 2 * i : 2 * i + 2, c * CHUNK : (c + 1) * CHUNK], res[:])
+
+        def store(cols):
+            for i, acc in enumerate(accs[cols.start]):
+                per_bank = acc.shape[1]
+                res = ring.tile(list(acc.shape), F32, name="res", bufs=7)
+                if cols.stop == T2:
+                    nc.vector.tensor_copy(res[:], acc[:])
+                else:
+                    nc.scalar.copy(res[:], acc[:])
+                nc.sync.dma_start(out_v[:, per_bank * i : per_bank * (i + 1), cols], res[:])
+
+        for cols in chunks:
+            page_max(both, 1, PACK - 1, cols)
+            second_stage(1, cols, both, radar_t)
+        for cols in chunks:
+            store(cols)

@@ -21,9 +21,10 @@ PACK = 4
 KP = P * PACK
 PASSES = 2
 WIDTHS = (256, 256, 256, 128, 128)
-PB_PAGES = 5
+EARLY = 2
+PB_PAGES = 6
 PA_PAGES = 2
-PB_OF = (0, 1, 2, 3, 4, 0, 1, 0)
+PB_OF = (0, 1, 2, 3, 4, 5, 0, 5)
 
 
 def tile_list_hail_severity_cells_kernel(
@@ -68,10 +69,14 @@ def tile_list_hail_severity_cells_kernel(
             return t
 
         def load_dealt(src, name):
-            t = keep.tile([P, PACK, S], F32, name=name)
-            for q in range(4):
-                nc.sync.dma_start(t[32 * q : 32 * q + 32], src.rearrange("(i t) j -> i t j", t=PACK))
-            return t
+            rows = src.rearrange("(i t) j -> i t j", t=PACK)
+            parts = []
+            for u in range(2):
+                t = keep.tile([P, 2, S], F32, name=name + "%d" % u)
+                for q in (0, 2, 1, 3):
+                    nc.sync.dma_start(t[32 * q : 32 * q + 32], rows[:, 2 * u : 2 * u + 2, :])
+                parts.append(t)
+            return parts
 
         def gathered(name):
             codes = [keep.tile([P, S], U32, name=name + "_codes%d" % a, align_bytes=64) for a in range(PASSES)]
@@ -99,8 +104,7 @@ def tile_list_hail_severity_cells_kernel(
         tab_s = zero_plane(T, "tab_s", nc.vector)
         wa_s = zero_plane(PASSES * N, "wa_s", nc.vector)
         pb = [keep.tile([P, T2], F32, name="pb%d" % i) for i in range(PB_PAGES)]
-        pa = [keep.tile([P, T2], F32, name="pa0")]
-        for page in pb + pa:
+        for page in pb:
             nc.vector.memset(page[:], 0.0)
 
         fall_v = [load_vector(fall[0:KP], "fall_v0", nc.gpsimd)]
@@ -112,9 +116,6 @@ def tile_list_hail_severity_cells_kernel(
         l4 = load_list(offs4, "l4")
         wg2_t = load_dealt(wg2, "wg2_t")
         w2_w.append(load_w2(1))
-        l1 = load_list(offs, "l1")
-        tab_w = [load_words(tab_words, a, slice(0, T), "tab_w%d" % a) for a in range(PASSES)]
-        load_packed_scales(tab_s, tab_scales, nc.sync)
 
         def load_rows(src, a, cols):
             raw = ring.tile([P, PACK, KP], F32, name="raw", bufs=3)
@@ -129,7 +130,7 @@ def tile_list_hail_severity_cells_kernel(
 
         def w1_part(b, a):
             raw = load_rows(w1, a, slice(b * KP, (b + 1) * KP))
-            grouped = ring.tile([P, PACK * KP], BF16, name="grouped", bufs=4, align_bytes=64)
+            grouped = ring.tile([P, PACK * KP], BF16, name="grouped", bufs=3, align_bytes=64)
             dst = grouped[:].rearrange("p (u e m j) -> p u m j e", u=2, e=2, j=PACK)
             src = raw[:].rearrange("p j (m u e) -> p u m j e", u=2, e=2)
             for u in range(2):
@@ -138,7 +139,7 @@ def tile_list_hail_severity_cells_kernel(
 
         def wz_part(b):
             raw = load_rows(wz, b, slice(0, N))
-            grouped = ring.tile([P, PACK * KP], BF16, name="grouped", bufs=4, align_bytes=64)
+            grouped = ring.tile([P, PACK * KP], BF16, name="grouped", bufs=3, align_bytes=64)
             nc.scalar.copy(
                 grouped[:].rearrange("p (c i j) -> p c j i", i=2, j=PACK),
                 raw[:].rearrange("p j (c i) -> p c j i", i=2),
@@ -181,7 +182,7 @@ def tile_list_hail_severity_cells_kernel(
             return h
 
         def place(page, lst, h, wg, t, js):
-            nc.vector.tensor_tensor(page[:].indirect(entries(lst, js)), h[:], wg[:, t, js], ALU.mult)
+            nc.vector.tensor_tensor(page[:].indirect(entries(lst, js)), h[:], wg[t // 2][:, t % 2, js], ALU.mult)
 
         def place_b(b, t, h, js):
             place(pb[PB_OF[PACK * b + t]], l4, h, wg2_t, t, js)
@@ -216,7 +217,7 @@ def tile_list_hail_severity_cells_kernel(
                 ALU.max,
             )
             size = ring.tile([P, PACK * width], BF16, name="size", bufs=3, align_bytes=64)
-            if b == PASSES - 1 and cols.start >= T2 // 2:
+            if b == PASSES - 1 and cols.stop == T2:
                 nc.vector.scalar_tensor_tensor(size[:], z[:], -1.0, z[:], ALU.mult, ALU.max)
             else:
                 nc.scalar.activation(size[:], z[:], ACT.Abs)
@@ -249,17 +250,22 @@ def tile_list_hail_severity_cells_kernel(
         gather(v2, tab2_w, tab2_s, l2, halves[1])
         place_b(0, 0, h_first, halves[0])
         place_b(0, 0, make_h2(0, 0, w2_d, halves[1], 1), halves[1])
-        pa.append(keep.tile([P, T2], F32, name="pa1", tag="tab2_w0", align_bytes=64))
-        nc.gpsimd.memset(pa[1][:], 0.0)
+        pa = [keep.tile([P, T2], F32, name="pa%d" % i, tag="tab2_w%d" % i, align_bytes=64) for i in range(PA_PAGES)]
+        for page in pa:
+            nc.gpsimd.memset(page[:], 0.0)
         for t in range(1, PACK):
             place_b(0, t, make_h2(0, t, w2_d, whole, t + 1), whole)
         w2_d = deal_w2(1)
+        w1_q = [[w1_part(0, a) for a in range(PASSES)]]
+        l1 = load_list(offs, "l1")
+        tab_w = [load_words(tab_words, a, slice(0, T), "tab_w%d" % a) for a in range(PASSES)]
+        load_packed_scales(tab_s, tab_scales, nc.sync)
         v1 = gathered("v1")
         gather(v1, tab_w, tab_s, l1, whole)
-
-        w1_q = [[w1_part(b, a) for a in range(PASSES)] for b in range(PASSES)]
         fall_v.append(load_vector(fall[KP:H], "fall_v1", nc.sync))
-        place_b(1, 0, make_h2(1, 0, w2_d, whole, 5), whole)
+        for t in range(EARLY):
+            place_b(1, t, make_h2(1, t, w2_d, whole, (5 + t) % 8), whole)
+        w1_q.append([w1_part(1, a) for a in range(PASSES)])
         b1_v = load_vector(b1, "b1_v", nc.sync)
         gain_v = load_vector(gain1, "gain_v", nc.sync)
         l3 = load_list(offs3, "l3")
@@ -267,15 +273,15 @@ def tile_list_hail_severity_cells_kernel(
 
         both = ring.tile([P, PACK, T2], F32, name="both", bufs=1)
         for t in range(PACK):
-            place_a(0, t, make_h1(0, t, w1_q[0], (6 + t) % 8))
+            place_a(0, t, make_h1(0, t, w1_q[0], (7 + t) % 8))
             page_max(both, 0, t)
-            if t + 2 < PACK:
-                place_b(1, t + 1, make_h2(1, t + 1, w2_d, whole, (6 + t) % 8), whole)
+            if t + EARLY < PACK - 1:
+                place_b(1, t + EARLY, make_h2(1, t + EARLY, w2_d, whole, (7 + t) % 8), whole)
         h2_last = make_h2(1, PACK - 1, w2_d, whole, 0)
 
-        h1 = [make_h1(1, t, w1_q[1], 2 + t) for t in range(PACK)]
-        radar_t = load_radar(0, "radar%d")
+        h1 = [make_h1(1, t, w1_q[1], 3 + t) for t in range(PACK)]
         wz_q = [wz_part(b) for b in range(PASSES)]
+        radar_t = load_radar(0, "radar%d")
         wa_w = keep.tile([P, PASSES, 2 * N], U8, name="wa_w", align_bytes=64)
         nc.sync.dma_start(wa_w[:].bitcast(I32), wa_words.rearrange("a p c -> p a c").bitcast(I32))
         for q in range(4):
@@ -310,15 +316,17 @@ def tile_list_hail_severity_cells_kernel(
         def store(cols):
             for i, acc in enumerate(accs[cols.start]):
                 per_bank = acc.shape[1]
-                res = ring.tile(list(acc.shape), F32, name="res", bufs=7)
+                res = ring.tile(list(acc.shape), F32, name="res", bufs=8)
                 if cols.stop == T2:
                     nc.vector.tensor_copy(res[:], acc[:])
                 else:
                     nc.scalar.copy(res[:], acc[:])
                 nc.sync.dma_start(out_v[:, per_bank * i : per_bank * (i + 1), cols], res[:])
 
-        for cols in chunks:
-            page_max(both, 1, PACK - 1, cols)
+        page_max(both, 1, PACK - 1, chunks[0])
+        for i, cols in enumerate(chunks):
+            if i + 1 < len(chunks):
+                page_max(both, 1, PACK - 1, chunks[i + 1])
             second_stage(1, cols, both, radar_t)
         for cols in chunks:
             store(cols)

@@ -68,15 +68,12 @@ def tile_list_hail_severity_cells_kernel(
             queue.dma_start(t[:], src.rearrange("(b p t) -> p b t", b=blocks, t=PACK))
             return t
 
-        def load_dealt(src, name):
+        def load_dealt(src, u, name):
             rows = src.rearrange("(i t) j -> i t j", t=PACK)
-            parts = []
-            for u in range(2):
-                t = keep.tile([P, 2, S], F32, name=name + "%d" % u)
-                for q in (0, 2, 1, 3):
-                    nc.sync.dma_start(t[32 * q : 32 * q + 32], rows[:, 2 * u : 2 * u + 2, :])
-                parts.append(t)
-            return parts
+            t = keep.tile([P, 2, S], F32, name=name + "%d" % u)
+            for q in (0, 2, 1, 3):
+                nc.sync.dma_start(t[32 * q : 32 * q + 32], rows[:, 2 * u : 2 * u + 2, :])
+            return t
 
         def gathered(name):
             codes = [keep.tile([P, S], U32, name=name + "_codes%d" % a, align_bytes=64) for a in range(PASSES)]
@@ -100,22 +97,23 @@ def tile_list_hail_severity_cells_kernel(
             return psum.tile(shape, F32, name="bank%d" % k, tag="bank%d" % k)
 
         tab2_s = zero_plane(TF, "tab2_s", nc.vector)
-        w2_s = zero_plane(H, "w2_s", nc.gpsimd)
+        w2_s = zero_plane(H, "w2_s", nc.vector)
         tab_s = zero_plane(T, "tab_s", nc.vector)
         wa_s = zero_plane(PASSES * N, "wa_s", nc.vector)
         pb = [keep.tile([P, T2], F32, name="pb%d" % i) for i in range(PB_PAGES)]
         for page in pb:
             nc.vector.memset(page[:], 0.0)
 
-        fall_v = [load_vector(fall[0:KP], "fall_v0", nc.gpsimd)]
+        fall_v = [load_vector(fall[0:KP], "fall_v0", nc.scalar)]
         l2 = load_list(offs2, "l2")
         tab2_w = [load_words(tab2_words, a, slice(0, TF), "tab2_w%d" % a) for a in range(PASSES)]
         load_packed_scales(tab2_s, tab2_scales, nc.scalar)
         w2_w = [load_w2(0)]
         load_packed_scales(w2_s, w2_scales, nc.scalar)
         l4 = load_list(offs4, "l4")
-        wg2_t = load_dealt(wg2, "wg2_t")
+        wg2_t = [load_dealt(wg2, 0, "wg2_t")]
         w2_w.append(load_w2(1))
+        wg2_t.append(load_dealt(wg2, 1, "wg2_t"))
 
         def load_rows(src, a, cols):
             raw = ring.tile([P, PACK, KP], F32, name="raw", bufs=3)
@@ -130,7 +128,8 @@ def tile_list_hail_severity_cells_kernel(
 
         def w1_part(b, a):
             raw = load_rows(w1, a, slice(b * KP, (b + 1) * KP))
-            grouped = ring.tile([P, PACK * KP], BF16, name="grouped", bufs=3, align_bytes=64)
+            tag = ("tab2_w%d", "grouped%d")[b] % a
+            grouped = keep.tile([P, PACK * KP], BF16, name="grouped_w1", tag=tag, align_bytes=64)
             dst = grouped[:].rearrange("p (u e m j) -> p u m j e", u=2, e=2, j=PACK)
             src = raw[:].rearrange("p j (m u e) -> p u m j e", u=2, e=2)
             for u in range(2):
@@ -139,10 +138,10 @@ def tile_list_hail_severity_cells_kernel(
 
         def wz_part(b):
             raw = load_rows(wz, b, slice(0, N))
-            grouped = ring.tile([P, PACK * KP], BF16, name="grouped", bufs=3, align_bytes=64)
+            grouped = keep.tile([P, PACK * KP], BF16, name="grouped_wz", tag="tab2_w%d" % b, align_bytes=64)
             nc.scalar.copy(
-                grouped[:].rearrange("p (c i j) -> p c j i", i=2, j=PACK),
-                raw[:].rearrange("p j (c i) -> p c j i", i=2),
+                grouped[:].rearrange("p (c i j) -> p c j i", i=4, j=PACK),
+                raw[:].rearrange("p j (c i) -> p c j i", i=4),
             )
             return quantise(grouped, N, "wz_%d" % b, keep, 1)
 
@@ -166,10 +165,13 @@ def tile_list_hail_severity_cells_kernel(
                     start=(a == 0), stop=(a == PASSES - 1),
                 )
 
-        def make_h2(b, t, w2_d, js, k):
+        def make_h2(b, t, w2_d, js, k, tag=None):
             acc = bank(k, [P, js.stop - js.start])
             first_product(acc, t, [(w2_d[0][a], w2_d[1][4 * a : P]) for a in range(PASSES)], v2, js)
-            h = ring.tile([P, js.stop - js.start], F32, name="h2", bufs=4)
+            if tag is None:
+                h = ring.tile([P, S], F32, name="h2", bufs=4)
+            else:
+                h = keep.tile([P, js.stop - js.start], F32, name="h2_half", tag=tag)
             nc.scalar.activation(h[:], acc[:], ACT.Copy, scale=fall_v[b][:, 0, t : t + 1])
             return h
 
@@ -211,9 +213,9 @@ def tile_list_hail_severity_cells_kernel(
             width = cols.stop - cols.start
             z = ring.tile([P, PACK * width], BF16, name="z", bufs=3, align_bytes=64)
             nc.vector.tensor_tensor(
-                z[:].rearrange("p (c i t) -> p c t i", i=2, t=PACK),
-                both[:, :, cols].rearrange("p t (c i) -> p c t i", i=2),
-                radar_t[cols.start // KP][:, :, cols.start % KP : cols.start % KP + width].rearrange("p t (c i) -> p c t i", i=2),
+                z[:].rearrange("p (c i t) -> p c t i", i=4, t=PACK),
+                both[:, :, cols].rearrange("p t (c i) -> p c t i", i=4),
+                radar_t[cols.start // KP][:, :, cols.start % KP : cols.start % KP + width].rearrange("p t (c i) -> p c t i", i=4),
                 ALU.max,
             )
             size = ring.tile([P, PACK * width], BF16, name="size", bufs=3, align_bytes=64)
@@ -246,11 +248,11 @@ def tile_list_hail_severity_cells_kernel(
         v2 = gathered("v2")
         gather(v2, tab2_w, tab2_s, l2, halves[0])
         w2_d = deal_w2(0)
-        h_first = make_h2(0, 0, w2_d, halves[0], 0)
+        h_first = make_h2(0, 0, w2_d, halves[0], 0, "pa0")
         gather(v2, tab2_w, tab2_s, l2, halves[1])
         place_b(0, 0, h_first, halves[0])
-        place_b(0, 0, make_h2(0, 0, w2_d, halves[1], 1), halves[1])
-        pa = [keep.tile([P, T2], F32, name="pa%d" % i, tag="tab2_w%d" % i, align_bytes=64) for i in range(PA_PAGES)]
+        place_b(0, 0, make_h2(0, 0, w2_d, halves[1], 1, "pa1"), halves[1])
+        pa = [keep.tile([P, T2], F32, name="pa%d" % i, tag="pa%d" % i) for i in range(PA_PAGES)]
         for page in pa:
             nc.gpsimd.memset(page[:], 0.0)
         for t in range(1, PACK):
@@ -269,7 +271,7 @@ def tile_list_hail_severity_cells_kernel(
         b1_v = load_vector(b1, "b1_v", nc.sync)
         gain_v = load_vector(gain1, "gain_v", nc.sync)
         l3 = load_list(offs3, "l3")
-        wg1_t = load_dealt(wg1, "wg1_t")
+        wg1_t = [load_dealt(wg1, u, "wg1_t") for u in range(2)]
 
         both = ring.tile([P, PACK, T2], F32, name="both", bufs=1)
         for t in range(PACK):

from contextlib import ExitStack

import concourse.mybir as mybir

K, H, N, T, TF, S, T2 = 1024, 1024, 512, 2048, 1024, 512, 1024
FLOPS = 2 * (2 * K * H * S + 2 * H * N * T2)

F32 = mybir.dt.float32
BF16 = mybir.dt.bfloat16
I32 = mybir.dt.int32
U32 = mybir.dt.uint32
U16 = mybir.dt.uint16
U8 = mybir.dt.uint8
E4M3 = mybir.dt.float8_e4m3fn_x4
E2M1 = mybir.dt.float4_e2m1fn_x4
ACT = mybir.ActivationFunctionType
ALU = mybir.AluOpType

P = 128
PACK = 4
KP = P * PACK
PASSES = 2
WIDTHS = (256, 256, 256, 128, 128)
EARLY = 2
PB_PAGES = 6
PA_PAGES = 2
PB_OF = (0, 1, 2, 3, 4, 5, 0, 5)


def tile_list_hail_severity_cells_kernel(
    tc, tab_words, tab_scales, tab2_words, tab2_scales, offs, offs2, offs3, offs4, w1, b1, gain1,
    w2_words, w2_scales, fall, wg1, wg2, radar, wz, wa_words, wa_scales, out,
):
    nc = tc.nc
    with ExitStack() as ctx:
        keep = ctx.enter_context(tc.tile_pool(name="keep", bufs=1))
        ring = ctx.enter_context(tc.tile_pool(name="ring", bufs=1))
        psum = ctx.enter_context(tc.psum_pool(name="psum", bufs=1))

        def load_list(src, name):
            t = keep.tile([P, S // 16], U16, name=name)
            nc.sync.dma_start(t[:], src)
            return t

        def load_words(src, a, cols, name):
            t = keep.tile([P, cols.stop - cols.start], U32, name=name, tag=name, align_bytes=64)
            nc.sync.dma_start(t[:].bitcast(I32), src[a].rearrange("p c i -> p (c i)").bitcast(I32)[:, cols])
            return t

        def load_w2(b):
            t = keep.tile([P, PASSES, KP], U32, name="w2_w%d" % b, align_bytes=64)
            words = w2_words.rearrange("a p c i -> p a (c i)").bitcast(I32)
            nc.sync.dma_start(t[:].bitcast(I32), words[:, :, b * KP : (b + 1) * KP])
            return t

        def zero_plane(width, name, engine):
            t = keep.tile([P, width], U8, name=name, align_bytes=64)
            engine.memset(t[:].bitcast(I32), 0)
            return t

        def load_packed_scales(t, src, queue):
            for q in range(4):
                queue.dma_start(t[32 * q : 32 * q + 8, :].bitcast(I32), src[:, 4 * q : 4 * q + 4, :].bitcast(I32))

        def load_vector(src, name, queue):
            blocks = src.shape[0] // KP
            t = keep.tile([P, blocks, PACK], F32, name=name)
            queue.dma_start(t[:], src.rearrange("(b p t) -> p b t", b=blocks, t=PACK))
            return t

        def load_dealt(src, u, name):
            rows = src.rearrange("(i t) j -> i t j", t=PACK)
            t = keep.tile([P, 2, S], F32, name=name + "%d" % u)
            for q in (0, 2, 1, 3):
                nc.sync.dma_start(t[32 * q : 32 * q + 32], rows[:, 2 * u : 2 * u + 2, :])
            return t

        def gathered(name):
            codes = [keep.tile([P, S], U32, name=name + "_codes%d" % a, align_bytes=64) for a in range(PASSES)]
            return codes, keep.tile([P, S], U8, name=name + "_scales", align_bytes=64)

        def entries(lst, js):
            return lst[:, js.start // 16 : js.stop // 16]

        def gather(dst, words, scales, lst, js):
            for a in range(PASSES):
                nc.vector.tensor_copy(dst[0][a][:, js], words[a][:].indirect(entries(lst, js)))
            nc.vector.tensor_copy(dst[1][:, js], scales[:].indirect(entries(lst, js)))

        def deal_columns(dst, src):
            nc.vector.tensor_copy(
                dst.rearrange("p (t c i) -> p c t i", t=PACK, i=4),
                src.rearrange("p (c i t) -> p c t i", t=PACK, i=4),
            )

        def bank(k, shape):
            return psum.tile(shape, F32, name="bank%d" % k, tag="bank%d" % k)

        tab2_s = zero_plane(TF, "tab2_s", nc.vector)
        w2_s = zero_plane(H, "w2_s", nc.vector)
        tab_s = zero_plane(T, "tab_s", nc.vector)
        wa_s = zero_plane(PASSES * N, "wa_s", nc.vector)
        pb = [keep.tile([P, T2], F32, name="pb%d" % i) for i in range(PB_PAGES)]
        for page in pb:
            nc.vector.memset(page[:], 0.0)

        fall_v = [load_vector(fall[0:KP], "fall_v0", nc.scalar)]
        l2 = load_list(offs2, "l2")
        tab2_w = [load_words(tab2_words, a, slice(0, TF), "tab2_w%d" % a) for a in range(PASSES)]
        load_packed_scales(tab2_s, tab2_scales, nc.scalar)
        w2_w = [load_w2(0)]
        load_packed_scales(w2_s, w2_scales, nc.scalar)
        l4 = load_list(offs4, "l4")
        wg2_t = [load_dealt(wg2, 0, "wg2_t")]
        w2_w.append(load_w2(1))
        wg2_t.append(load_dealt(wg2, 1, "wg2_t"))

        def load_rows(src, a, cols):
            raw = ring.tile([P, PACK, KP], F32, name="raw", bufs=3)
            nc.sync.dma_start(raw[:], src[a * KP : (a + 1) * KP, cols].rearrange("(p j) c -> p j c", j=PACK))
            return raw

        def quantise(grouped, width, name, pool, bufs):
            codes = pool.tile([P, width], U32, name=name + "_codes", align_bytes=64, bufs=bufs)
            scales = pool.tile([P, width], U8, name=name + "_scales", align_bytes=64, bufs=bufs)
            nc.vector.quantize_mx(out=codes[:].bitcast(E4M3), scales=scales[:], in_=grouped[:])
            return codes, scales

        def w1_part(b, a):
            raw = load_rows(w1, a, slice(b * KP, (b + 1) * KP))
            tag = ("tab2_w%d", "grouped%d")[b] % a
            grouped = keep.tile([P, PACK * KP], BF16, name="grouped_w1", tag=tag, align_bytes=64)
            dst = grouped[:].rearrange("p (u e m j) -> p u m j e", u=2, e=2, j=PACK)
            src = raw[:].rearrange("p j (m u e) -> p u m j e", u=2, e=2)
            for u in range(2):
                nc.scalar.copy(dst[:, u], src[:, u])
            return quantise(grouped, KP, "w1_%d%d" % (b, a), keep, 1)

        def wz_part(b):
            raw = load_rows(wz, b, slice(0, N))
            grouped = keep.tile([P, PACK * KP], BF16, name="grouped_wz", tag="tab2_w%d" % b, align_bytes=64)
            nc.scalar.copy(
                grouped[:].rearrange("p (c i j) -> p c j i", i=4, j=PACK),
                raw[:].rearrange("p j (c i) -> p c j i", i=4),
            )
            return quantise(grouped, N, "wz_%d" % b, keep, 1)

        def deal_w2(b):
            codes = []
            for a in range(PASSES):
                d = keep.tile([P, KP], U32, name="w2_d%d%d" % (b, a), align_bytes=64)
                deal_columns(d[:], w2_w[b][:, a, :])
                codes.append(d)
            ds = keep.tile([P, KP], U8, name="w2_ds%d" % b, align_bytes=64)
            deal_columns(ds[:], w2_s[:, b * KP : (b + 1) * KP])
            return codes, ds

        def first_product(acc, t, lhs, rhs, js):
            cols = slice(t * P, (t + 1) * P)
            for a in range(PASSES):
                codes, scales = lhs[a]
                nc.tensor.matmul_mx(
                    out=acc[:], lhsT=codes[:, cols].bitcast(E4M3), lhsT_scale=scales[:, cols],
                    rhs=rhs[0][a][:, js].bitcast(E4M3), rhs_scale=rhs[1][4 * a : P, js],
                    start=(a == 0), stop=(a == PASSES - 1),
                )

        def make_h2(b, t, w2_d, js, k, tag=None):
            acc = bank(k, [P, js.stop - js.start])
            first_product(acc, t, [(w2_d[0][a], w2_d[1][4 * a : P]) for a in range(PASSES)], v2, js)
            if tag is None:
                h = ring.tile([P, S], F32, name="h2", bufs=4)
            else:
                h = keep.tile([P, js.stop - js.start], F32, name="h2_half", tag=tag)
            nc.scalar.activation(h[:], acc[:], ACT.Copy, scale=fall_v[b][:, 0, t : t + 1])
            return h

        def make_h1(b, t, w1_q, k):
            acc = bank(k, [P, S])
            first_product(acc, t, w1_q, v1, whole)
            h = ring.tile([P, S], F32, name="h1", bufs=5)
            nc.scalar.activation(h[:], acc[:], ACT.Tanh, bias=b1_v[:, b, t : t + 1])
            nc.scalar.activation(h[:], h[:], ACT.Copy, scale=gain_v[:, b, t : t + 1])
            return h

        def place(page, lst, h, wg, t, js):
            nc.vector.tensor_tensor(page[:].indirect(entries(lst, js)), h[:], wg[t // 2][:, t % 2, js], ALU.mult)

        def place_b(b, t, h, js):
            place(pb[PB_OF[PACK * b + t]], l4, h, wg2_t, t, js)

        def place_a(b, t, h):
            place(pa[(PACK * b + t) % PA_PAGES], l3, h, wg1_t, t, whole)

        def page_max(both, b, t, cols=slice(0, T2)):
            s = PACK * b + t
            nc.vector.tensor_tensor(both[:, t, cols], pa[s % PA_PAGES][:, cols], pb[PB_OF[s]][:, cols], ALU.max)

        def load_radar(b, tags):
            parts = []
            for i in range(2):
                r = keep.tile([P, PACK, KP], F32, name="radar%d%d" % (b, i), tag=tags % i, align_bytes=64)
                rows = radar[b * KP : (b + 1) * KP, i * KP : (i + 1) * KP]
                nc.sync.dma_start(r[:], rows.rearrange("(p j) m -> p j m", j=PACK))
                parts.append(r)
            return parts

        def target(cols, g):
            per_bank = KP // (cols.stop - cols.start)
            return accs[cols.start][g // per_bank][:, g % per_bank, :], g % per_bank == 0, g % per_bank == per_bank - 1

        def second_stage(b, cols, both, radar_t):
            width = cols.stop - cols.start
            z = ring.tile([P, PACK * width], BF16, name="z", bufs=3, align_bytes=64)
            nc.vector.tensor_tensor(
                z[:].rearrange("p (c i t) -> p c t i", i=4, t=PACK),
                both[:, :, cols].rearrange("p t (c i) -> p c t i", i=4),
                radar_t[cols.start // KP][:, :, cols.start % KP : cols.start % KP + width].rearrange("p t (c i) -> p c t i", i=4),
                ALU.max,
            )
            size = ring.tile([P, PACK * width], BF16, name="size", bufs=3, align_bytes=64)
            if b == PASSES - 1 and cols.stop == T2:
                nc.vector.scalar_tensor_tensor(size[:], z[:], -1.0, z[:], ALU.mult, ALU.max)
            else:
                nc.scalar.activation(size[:], z[:], ACT.Abs)
            zq = quantise(z, width, "zq", ring, 3)
            for g in range(N // P):
                acc, first, last = target(cols, g)
                nc.tensor.matmul_mx(
                    out=acc,
                    lhsT=wz_q[b][0][:, g * P : (g + 1) * P].bitcast(E4M3), lhsT_scale=wz_q[b][1][:, g * P : (g + 1) * P],
                    rhs=zq[0][:].bitcast(E4M3), rhs_scale=zq[1][:],
                    start=(b == 0 and first), stop=False,
                )
            sq = quantise(size, width, "sq", ring, 3)
            for g in range(N // P):
                acc, first, last = target(cols, g)
                nc.tensor.matmul_mx(
                    out=acc,
                    lhsT=wa_w[:, b, 2 * g * P : 2 * (g + 1) * P].bitcast(E2M1),
                    lhsT_scale=wa_s[:, b * N + g * P : b * N + (g + 1) * P],
                    rhs=sq[0][:].bitcast(E4M3), rhs_scale=sq[1][:],
                    start=False, stop=(b == PASSES - 1 and last),
                )

        whole = slice(0, S)
        halves = [slice(0, S // 2), slice(S // 2, S)]
        v2 = gathered("v2")
        gather(v2, tab2_w, tab2_s, l2, halves[0])
        w2_d = deal_w2(0)
        h_first = make_h2(0, 0, w2_d, halves[0], 0, "pa0")
        gather(v2, tab2_w, tab2_s, l2, halves[1])
        place_b(0, 0, h_first, halves[0])
        place_b(0, 0, make_h2(0, 0, w2_d, halves[1], 1, "pa1"), halves[1])
        pa = [keep.tile([P, T2], F32, name="pa%d" % i, tag="pa%d" % i) for i in range(PA_PAGES)]
        for page in pa:
            nc.gpsimd.memset(page[:], 0.0)
        for t in range(1, PACK):
            place_b(0, t, make_h2(0, t, w2_d, whole, t + 1), whole)
        w2_d = deal_w2(1)
        w1_q = [[w1_part(0, a) for a in range(PASSES)]]
        l1 = load_list(offs, "l1")
        tab_w = [load_words(tab_words, a, slice(0, T), "tab_w%d" % a) for a in range(PASSES)]
        load_packed_scales(tab_s, tab_scales, nc.sync)
        v1 = gathered("v1")
        gather(v1, tab_w, tab_s, l1, whole)
        fall_v.append(load_vector(fall[KP:H], "fall_v1", nc.sync))
        for t in range(EARLY):
            place_b(1, t, make_h2(1, t, w2_d, whole, (5 + t) % 8), whole)
        w1_q.append([w1_part(1, a) for a in range(PASSES)])
        b1_v = load_vector(b1, "b1_v", nc.sync)
        gain_v = load_vector(gain1, "gain_v", nc.sync)
        l3 = load_list(offs3, "l3")
        wg1_t = [load_dealt(wg1, u, "wg1_t") for u in range(2)]

        both = ring.tile([P, PACK, T2], F32, name="both", bufs=1)
        for t in range(PACK):
            place_a(0, t, make_h1(0, t, w1_q[0], (7 + t) % 8))
            page_max(both, 0, t)
            if t + EARLY < PACK - 1:
                place_b(1, t + EARLY, make_h2(1, t + EARLY, w2_d, whole, (7 + t) % 8), whole)
        h2_last = make_h2(1, PACK - 1, w2_d, whole, 0)

        h1 = [make_h1(1, t, w1_q[1], 3 + t) for t in range(PACK)]
        wz_q = [wz_part(b) for b in range(PASSES)]
        radar_t = load_radar(0, "radar%d")
        wa_w = keep.tile([P, PASSES, 2 * N], U8, name="wa_w", align_bytes=64)
        nc.sync.dma_start(wa_w[:].bitcast(I32), wa_words.rearrange("a p c -> p a c").bitcast(I32))
        for q in range(4):
            nc.sync.dma_start(
                wa_s[32 * q : 32 * q + 4, :].rearrange("r (a c) -> r a c", a=PASSES).bitcast(I32),
                wa_scales[:, 4 * q : 4 * q + 4, :].rearrange("a r c -> r a c").bitcast(I32),
            )

        place_a(1, 0, h1[0])
        chunks = []
        accs = {}
        for width in WIDTHS:
            start = chunks[-1].stop if chunks else 0
            chunks.append(slice(start, start + width))
            per_bank = KP // width
            accs[start] = [bank(start // P + i, [P, per_bank, width]) for i in range(N // P // per_bank)]
        for cols in chunks:
            second_stage(0, cols, both, radar_t)

        radar_t = load_radar(1, "tab_w%d")
        both = ring.tile([P, PACK, T2], F32, name="both", bufs=1)
        place_a(1, 1, h1[1])
        page_max(both, 1, 0)
        page_max(both, 1, 1)
        place_a(1, 2, h1[2])
        place_b(1, 3, h2_last, whole)
        page_max(both, 1, 2)
        place_a(1, 3, h1[3])

        out_v = out.rearrange("(g p) m -> p g m", p=P)

        def store(cols):
            for i, acc in enumerate(accs[cols.start]):
                per_bank = acc.shape[1]
                res = ring.tile(list(acc.shape), F32, name="res", bufs=8)
                if cols.stop == T2:
                    nc.vector.tensor_copy(res[:], acc[:])
                else:
                    nc.scalar.copy(res[:], acc[:])
                nc.sync.dma_start(out_v[:, per_bank * i : per_bank * (i + 1), cols], res[:])

        page_max(both, 1, PACK - 1, chunks[0])
        for i, cols in enumerate(chunks):
            if i + 1 < len(chunks):
                page_max(both, 1, PACK - 1, chunks[i + 1])
            second_stage(1, cols, both, radar_t)
        for cols in chunks:
            store(cols)
